import numpy as np
import ml_dtypes


def mxq(x, axis, fmt="e4m3"):
    dtype, down = {"e4m3": (ml_dtypes.float8_e4m3fn, 7), "e5m2": (ml_dtypes.float8_e5m2, 14)}[fmt]
    v = np.moveaxis(np.asarray(x, np.float32).astype(ml_dtypes.bfloat16).astype(np.float64), axis, -1)
    blocks = v.reshape(v.shape[:-1] + (-1, 32))
    amax = np.abs(blocks).max(-1, keepdims=True)
    byte = np.maximum(np.where(amax > 0, np.frexp(amax)[1] - 1 + 127, 0) - down, 1)
    scale = np.exp2(byte - 127.0)
    codes = (blocks / scale).astype(np.float32).astype(dtype).astype(np.float64)
    return np.moveaxis((codes * scale).reshape(v.shape), -1, axis)


WIDE = False


def mx_kscale(k):
    if not WIDE:
        return np.ones(k)
    levels = np.array([30, -30])
    if k % 512:
        return np.exp2(np.random.permutation(np.resize(levels, k // 32))).repeat(32)
    a = np.empty((k // 512, 16))
    for p in range(k // 512):
        a[p, :8] = np.random.permutation(np.resize(levels, 8))
        for g in range(8):
            far = levels[np.abs(levels - a[p, g]) >= 10]
            a[p, g + 8] = far[np.random.randint(len(far))]
    return np.exp2(a.ravel()).repeat(32)


def f64(x):
    return np.asarray(x).astype(np.float64)


def striped(idx):
    return np.tile(np.asarray(idx).reshape(-1, 16).T, (8, 1)).astype(np.uint16)


def unstriped(offs):
    return offs[:16].T.reshape(-1).astype(np.int64)


E2M1 = np.array([0.0, 0.5, 1.0, 1.5, 2.0, 3.0, 4.0, 6.0, -0.0, -0.5, -1.0, -1.5, -2.0, -3.0, -4.0, -6.0])


def pack_weight(w, fmt):
    k, n = w.shape
    w = f64(np.asarray(w, np.float32).astype(ml_dtypes.bfloat16)).reshape(k // 32, 32, n)
    amax = np.abs(w).max(1)
    if fmt in ("e4m3", "e5m2"):
        byte = np.frexp(amax)[1] - 1 + 127 - (7 if fmt == "e4m3" else 14)
    else:
        mant, ex = np.frexp(amax / 6.0)
        byte = np.where(mant > 0.5, ex, ex - 1) + 127
    byte = np.clip(np.where(amax > 0, byte, 1), 1, 254)
    scaled = (w * np.exp2(127.0 - byte)[:, None, :]).reshape(k, n).astype(np.float32)
    by_word = np.ascontiguousarray(scaled.reshape(k // 512, 128, 4, n).transpose(0, 1, 3, 2))
    if fmt in ("e4m3", "e5m2"):
        words = by_word.astype(ml_dtypes.float8_e4m3fn if fmt == "e4m3" else ml_dtypes.float8_e5m2).view(np.uint8)
    else:
        c = by_word.astype(ml_dtypes.float4_e2m1fn).view(np.uint8) & 0xF
        words = (c[..., 0::2] | (c[..., 1::2] << 4)).reshape(k // 512, 128, 2 * n)
    return np.ascontiguousarray(words), np.ascontiguousarray(byte.astype(np.uint8).reshape(k // 512, 16, n))


def unpack_weight(words, scales, fmt):
    g, _, n = scales.shape
    words = np.ascontiguousarray(words).reshape(g, 128, n, -1)
    if fmt in ("e4m3", "e5m2"):
        vals = words.view(ml_dtypes.float8_e4m3fn if fmt == "e4m3" else ml_dtypes.float8_e5m2).astype(np.float64)
    else:
        nib = np.empty((g, 128, n, 4), np.uint8)
        nib[..., 0::2] = words & 0xF
        nib[..., 1::2] = words >> 4
        vals = E2M1[nib]
    vals = vals * np.repeat(np.exp2(scales.astype(np.float64) - 127.0), 8, axis=1)[..., None]
    return vals.transpose(0, 1, 3, 2).reshape(g * 512, n)


K, T, J, N, G = 1024, 1024, 256, 256, 32


def setup_inputs():
    n = np.random.standard_normal
    idx = np.random.permutation(T)[:J]
    fk = mx_kscale(K)
    xtp = pack_weight(n((K, T)) * np.random.uniform(0.4, 1.6, (1, T)) / fk[:, None], "e5m2")
    wap = pack_weight(n((K, N)) * 1 / np.sqrt(K) * fk[:, None], "e4m3")
    return {
        "xt_words": xtp[0],
        "xt_scales": xtp[1],
        "wa_words": wap[0],
        "wa_scales": wap[1],
        "wb": (n((K, N)) * 1 / np.sqrt(K) * fk[:, None]).astype(np.float32),
        "bi": (np.random.uniform(-0.6, 0.6, (1, N))).astype(np.float32),
        "offs": striped(idx),
    }


def reference(xt_words, xt_scales, wa_words, wa_scales, wb, bi, offs):
    idx = unstriped(offs)
    xtu = unpack_weight(xt_words, xt_scales, "e5m2")
    wau = unpack_weight(wa_words, wa_scales, "e4m3")
    xtidxg = xtu[:, idx]
    a = xtidxg.T @ wau
    wbq = mxq(f64(wb), 0, "e4m3")
    b0 = xtidxg.T @ wbq
    b2 = b0 + f64(bi)
    g1 = a.reshape(J, G, N // G).mean(axis=2)
    g2 = np.repeat(g1, N // G, axis=1)
    y = (a - g2) * np.abs(b2)
    return y

@@ -1,0 +1,138 @@
+from contextlib import ExitStack
+
+import concourse.mybir as mybir
+from concourse.masks import make_identity
+
+K, T, J, N, G = 1024, 1024, 256, 256, 32
+FLOPS = 2 * 2 * K * J * N
+
+F32 = mybir.dt.float32
+BF16 = mybir.dt.bfloat16
+I32 = mybir.dt.int32
+U32 = mybir.dt.uint32
+U16 = mybir.dt.uint16
+U8 = mybir.dt.uint8
+E4M3 = mybir.dt.float8_e4m3fn_x4
+E5M2 = mybir.dt.float8_e5m2_x4
+ALU = mybir.AluOpType
+ACT = mybir.ActivationFunctionType
+
+P = 128
+PACK = 4
+PASSES = K // (P * PACK)
+HALVES = 2
+QUADS = 4
+GROUP = N // G
+
+
+def tile_list_rows_onetoken_groupcentred_kernel(tc, xt_words, xt_scales, wa_words, wa_scales, wb, bi, offs, out):
+    nc = tc.nc
+    with ExitStack() as ctx:
+        sb = ctx.enter_context(tc.tile_pool(name="sb", bufs=1))
+        ps = ctx.enter_context(tc.psum_pool(name="ps", bufs=1))
+
+        offsets = sb.tile([P, J // 16], U16, name="offsets")
+        xs = sb.tile([P, PASSES * T], U8, name="xs", align_bytes=64)
+        was = sb.tile([P, PASSES * N], U8, name="was", align_bytes=64)
+        xw = [sb.tile([P, T], U32, name="xw%d" % z, align_bytes=64) for z in range(PASSES)]
+        waw = sb.tile([P, PASSES * N], U32, name="waw", align_bytes=64)
+        raw = [sb.tile([P, PACK, N], F32, name="raw%d" % z, align_bytes=64) for z in range(PASSES)]
+        brow = sb.tile([P, P], F32, name="brow")
+        ident = sb.tile([P, P], F32, name="ident")
+
+        nc.vector.memset(xs[:].bitcast(I32), 0)
+        nc.vector.memset(was[:].bitcast(I32), 0)
+        nc.gpsimd.memset(brow[:], 0.0)
+        make_identity(nc, ident[:])
+
+        def load_scales(plane, src):
+            for q in range(QUADS):
+                nc.sync.dma_start(
+                    out=plane[32 * q : 32 * q + 4, :].bitcast(I32).rearrange("r (z c) -> r z c", z=PASSES),
+                    in_=src[:, 4 * q : 4 * q + 4, :].rearrange("z r c -> r z c").bitcast(I32),
+                )
+
+        nc.sync.dma_start(offsets[:], offs)
+        for z in range(PASSES):
+            nc.sync.dma_start(out=raw[z][:], in_=wb[z * 512 : (z + 1) * 512, :].rearrange("(p t) n -> p t n", t=PACK))
+        load_scales(xs, xt_scales)
+        for z in range(PASSES):
+            nc.sync.dma_start(out=xw[z][:].bitcast(I32), in_=xt_words[z].rearrange("p c t -> p (c t)").bitcast(I32))
+        load_scales(was, wa_scales)
+        nc.sync.dma_start(out=brow[0:HALVES, :], in_=bi.rearrange("o (h p) -> (o h) p", h=HALVES))
+        nc.sync.dma_start(
+            out=waw[:].bitcast(I32).rearrange("p (z c) -> p z c", z=PASSES),
+            in_=wa_words.rearrange("z p c t -> p z (c t)").bitcast(I32),
+        )
+
+        wbw, wbs, xgw, xgs = [], [], [], []
+        for z in range(PASSES):
+            plane = sb.tile([P, J], U8, name="xgs%d" % z, align_bytes=64)
+            nc.vector.tensor_copy(plane[:], xs[:, z * T : (z + 1) * T].indirect(offsets[:]))
+            xgs.append(plane)
+        for z in range(PASSES):
+            grouped = sb.tile([P, N, PACK], BF16, name="grouped%d" % z, align_bytes=64)
+            nc.scalar.activation(
+                grouped[:].rearrange("p (c i) t -> p c t i", i=4),
+                raw[z][:].rearrange("p t (c i) -> p c t i", i=4),
+                ACT.Copy,
+            )
+            codes = sb.tile([P, N], U32, name="wbw%d" % z, align_bytes=64)
+            plane = sb.tile([P, N], U8, name="wbs%d" % z, align_bytes=64)
+            nc.vector.quantize_mx(out=codes[:].bitcast(E4M3), scales=plane[:], in_=grouped[:].rearrange("p n t -> p (n t)"))
+            wbw.append(codes)
+            wbs.append(plane)
+        for z in range(PASSES):
+            words = sb.tile([P, J], U32, name="xgw%d" % z, align_bytes=64)
+            nc.vector.tensor_copy(words[:], xw[z][:].indirect(offsets[:]))
+            xgw.append(words)
+
+        bias_ps = ps.tile([P, P], F32, name="bias_ps")
+        nc.tensor.transpose(bias_ps[:], brow[:], ident[:])
+        bcol = sb.tile([P, HALVES], F32, name="bcol")
+        nc.scalar.copy(bcol[:], bias_ps[:, 0:HALVES])
+
+        bT = [ps.tile([P, J], F32, name="bT%d" % h) for h in range(HALVES)]
+        acc = [ps.tile([P, N], F32, name="acc%d" % h) for h in range(HALVES)]
+        for z in range(PASSES):
+            for h in range(HALVES):
+                cols = slice(h * P, (h + 1) * P)
+                nc.tensor.matmul_mx(
+                    out=bT[h][:], lhsT=wbw[z][:, cols].bitcast(E4M3), lhsT_scale=wbs[z][:, cols],
+                    rhs=xgw[z][:].bitcast(E5M2), rhs_scale=xgs[z][:], start=(z == 0), stop=(z == PASSES - 1),
+                )
+        for h in range(HALVES):
+            cols = slice(h * P, (h + 1) * P)
+            for z in range(PASSES):
+                wcols = slice(z * N, (z + 1) * N)
+                nc.tensor.matmul_mx(
+                    out=acc[h][:], lhsT=xgw[z][:, cols].bitcast(E5M2), lhsT_scale=xgs[z][:, cols],
+                    rhs=waw[:, wcols].bitcast(E4M3), rhs_scale=was[:, wcols], start=(z == 0), stop=(z == PASSES - 1),
+                )
+
+        magT = []
+        for h in range(HALVES):
+            m = sb.tile([P, J], F32, name="magT%d" % h)
+            nc.scalar.activation(m[:], bT[h][:], ACT.Abs, bias=bcol[:, h : h + 1])
+            magT.append(m)
+        mag = [ps.tile([P, N], F32, name="mag%d" % h) for h in range(HALVES)]
+        for jt in range(HALVES):
+            for h in range(HALVES):
+                nc.tensor.transpose(mag[jt][:, h * P : (h + 1) * P], magT[h][:, jt * P : (jt + 1) * P], ident[:])
+
+        sums, centred = [], []
+        for jt in range(HALVES):
+            s = sb.tile([P, G], F32, name="sums%d" % jt)
+            nc.vector.tensor_reduce(s[:], acc[jt][:].rearrange("p (g i) -> p g i", i=GROUP), mybir.AxisListType.X, ALU.add)
+            sums.append(s)
+        for jt in range(HALVES):
+            c = sb.tile([P, G, GROUP], F32, name="centred%d" % jt)
+            nc.vector.scalar_tensor_tensor(
+                c[:], sums[jt][:].unsqueeze(2).to_broadcast([P, G, GROUP]), -1.0 / GROUP,
+                acc[jt][:].rearrange("p (g i) -> p g i", i=GROUP), ALU.mult, ALU.add,
+            )
+            centred.append(c)
+        for jt in range(HALVES):
+            y = sb.tile([P, N], F32, name="y%d" % jt)
+            nc.vector.tensor_tensor(y[:], centred[jt][:].rearrange("p g i -> p (g i)"), mag[jt][:], ALU.mult)
+            nc.sync.dma_start(out=out[jt * P : (jt + 1) * P, :], in_=y[:])

@@ -35,14 +35,13 @@ def tile_list_rows_onetoken_groupcentred_kernel(tc, xt_words, xt_scales, wa_word
         xs = sb.tile([P, PASSES * T], U8, name="xs", align_bytes=64)
         was = sb.tile([P, PASSES * N], U8, name="was", align_bytes=64)
         xw = [sb.tile([P, T], U32, name="xw%d" % z, align_bytes=64) for z in range(PASSES)]
-        waw = sb.tile([P, PASSES * N], U32, name="waw", align_bytes=64)
+        waw = [sb.tile([P, N], U32, name="waw%d" % z, align_bytes=64) for z in range(PASSES)]
         raw = [sb.tile([P, PACK, N], F32, name="raw%d" % z, align_bytes=64) for z in range(PASSES)]
-        brow = sb.tile([P, P], F32, name="brow")
+        bcol = sb.tile([P, HALVES, 8], F32, name="bcol")
         ident = sb.tile([P, P], F32, name="ident")
 
-        nc.vector.memset(xs[:].bitcast(I32), 0)
+        nc.gpsimd.memset(xs[:].bitcast(I32), 0)
         nc.vector.memset(was[:].bitcast(I32), 0)
-        nc.gpsimd.memset(brow[:], 0.0)
         make_identity(nc, ident[:])
 
         def load_scales(plane, src):
@@ -52,24 +51,34 @@ def tile_list_rows_onetoken_groupcentred_kernel(tc, xt_words, xt_scales, wa_word
                     in_=src[:, 4 * q : 4 * q + 4, :].rearrange("z r c -> r z c").bitcast(I32),
                 )
 
-        nc.sync.dma_start(offsets[:], offs)
-        for z in range(PASSES):
-            nc.sync.dma_start(out=raw[z][:], in_=wb[z * 512 : (z + 1) * 512, :].rearrange("(p t) n -> p t n", t=PACK))
-        load_scales(xs, xt_scales)
-        for z in range(PASSES):
+        def load_words(z):
             nc.sync.dma_start(out=xw[z][:].bitcast(I32), in_=xt_words[z].rearrange("p c t -> p (c t)").bitcast(I32))
-        load_scales(was, wa_scales)
-        nc.sync.dma_start(out=brow[0:HALVES, :], in_=bi.rearrange("o (h p) -> (o h) p", h=HALVES))
-        nc.sync.dma_start(
-            out=waw[:].bitcast(I32).rearrange("p (z c) -> p z c", z=PASSES),
-            in_=wa_words.rearrange("z p c t -> p z (c t)").bitcast(I32),
-        )
 
-        wbw, wbs, xgw, xgs = [], [], [], []
+        def load_wa(z):
+            nc.sync.dma_start(out=waw[z][:].bitcast(I32), in_=wa_words[z].rearrange("p c t -> p (c t)").bitcast(I32))
+
+        def load_wb(z):
+            nc.sync.dma_start(out=raw[z][:], in_=wb[z * 512 : (z + 1) * 512, :].rearrange("(p t) n -> p t n", t=PACK))
+
+        nc.sync.dma_start(offsets[:], offs)
+        with nc.allow_non_contiguous_dma(reason="one bias value a partition"):
+            nc.scalar.dma_start(out=bcol[:, :, 0:1], in_=bi.rearrange("o (h p) -> p h o", h=HALVES))
+        load_wb(0)
+        load_scales(xs, xt_scales)
+        load_wb(1)
+        load_words(0)
+        load_wa(0)
+        load_scales(was, wa_scales)
+        load_words(1)
+        load_wa(1)
+
+        wbw, wbs, xgs = [], [], []
         for z in range(PASSES):
             plane = sb.tile([P, J], U8, name="xgs%d" % z, align_bytes=64)
             nc.vector.tensor_copy(plane[:], xs[:, z * T : (z + 1) * T].indirect(offsets[:]))
             xgs.append(plane)
+        bT = [[ps.tile([P, P], F32, name="bT%d%d" % (jt, h)) for h in range(HALVES)] for jt in range(HALVES)]
+        acc = [ps.tile([P, N], F32, name="acc%d" % jt) for jt in range(HALVES)]
         for z in range(PASSES):
             grouped = sb.tile([P, N, PACK], BF16, name="grouped%d" % z, align_bytes=64)
             nc.scalar.activation(
@@ -82,43 +91,30 @@ def tile_list_rows_onetoken_groupcentred_kernel(tc, xt_words, xt_scales, wa_word
             nc.vector.quantize_mx(out=codes[:].bitcast(E4M3), scales=plane[:], in_=grouped[:].rearrange("p n t -> p (n t)"))
             wbw.append(codes)
             wbs.append(plane)
-        for z in range(PASSES):
-            words = sb.tile([P, J], U32, name="xgw%d" % z, align_bytes=64)
-            nc.vector.tensor_copy(words[:], xw[z][:].indirect(offsets[:]))
-            xgw.append(words)
-
-        bias_ps = ps.tile([P, P], F32, name="bias_ps")
-        nc.tensor.transpose(bias_ps[:], brow[:], ident[:])
-        bcol = sb.tile([P, HALVES], F32, name="bcol")
-        nc.scalar.copy(bcol[:], bias_ps[:, 0:HALVES])
-
-        bT = [ps.tile([P, J], F32, name="bT%d" % h) for h in range(HALVES)]
-        acc = [ps.tile([P, N], F32, name="acc%d" % h) for h in range(HALVES)]
-        for z in range(PASSES):
-            for h in range(HALVES):
-                cols = slice(h * P, (h + 1) * P)
+            wcols = slice(z * N, (z + 1) * N)
+            for jt in range(HALVES):
+                jcols = slice(jt * P, (jt + 1) * P)
+                words = sb.tile([P, P], U32, name="xgw%d%d" % (z, jt), align_bytes=64)
+                nc.vector.tensor_copy(words[:], xw[z][:].indirect(offsets[:, jt * 8 : (jt + 1) * 8]))
+                for h in range(HALVES):
+                    cols = slice(h * P, (h + 1) * P)
+                    nc.tensor.matmul_mx(
+                        out=bT[jt][h][:], lhsT=wbw[z][:, cols].bitcast(E4M3), lhsT_scale=wbs[z][:, cols],
+                        rhs=words[:].bitcast(E5M2), rhs_scale=xgs[z][:, jcols], start=(z == 0), stop=(z == PASSES - 1),
+                    )
                 nc.tensor.matmul_mx(
-                    out=bT[h][:], lhsT=wbw[z][:, cols].bitcast(E4M3), lhsT_scale=wbs[z][:, cols],
-                    rhs=xgw[z][:].bitcast(E5M2), rhs_scale=xgs[z][:], start=(z == 0), stop=(z == PASSES - 1),
-                )
-        for h in range(HALVES):
-            cols = slice(h * P, (h + 1) * P)
-            for z in range(PASSES):
-                wcols = slice(z * N, (z + 1) * N)
-                nc.tensor.matmul_mx(
-                    out=acc[h][:], lhsT=xgw[z][:, cols].bitcast(E5M2), lhsT_scale=xgs[z][:, cols],
-                    rhs=waw[:, wcols].bitcast(E4M3), rhs_scale=was[:, wcols], start=(z == 0), stop=(z == PASSES - 1),
+                    out=acc[jt][:], lhsT=words[:].bitcast(E5M2), lhsT_scale=xgs[z][:, jcols],
+                    rhs=waw[z][:].bitcast(E4M3), rhs_scale=was[:, wcols], start=(z == 0), stop=(z == PASSES - 1),
                 )
 
-        magT = []
-        for h in range(HALVES):
-            m = sb.tile([P, J], F32, name="magT%d" % h)
-            nc.scalar.activation(m[:], bT[h][:], ACT.Abs, bias=bcol[:, h : h + 1])
-            magT.append(m)
-        mag = [ps.tile([P, N], F32, name="mag%d" % h) for h in range(HALVES)]
+        mag = []
         for jt in range(HALVES):
+            turned = ps.tile([P, N], F32, name="mag%d" % jt, tag="mag%d" % jt)
             for h in range(HALVES):
-                nc.tensor.transpose(mag[jt][:, h * P : (h + 1) * P], magT[h][:, jt * P : (jt + 1) * P], ident[:])
+                m = sb.tile([P, P], F32, name="magT%d%d" % (jt, h))
+                nc.scalar.activation(m[:], bT[jt][h][:], ACT.Abs, bias=bcol[:, h, 0:1])
+                nc.tensor.transpose(turned[:, h * P : (h + 1) * P], m[:], ident[:])
+            mag.append(turned)
 
         sums, centred = [], []
         for jt in range(HALVES):

@@ -37,18 +37,19 @@ def tile_list_rows_onetoken_groupcentred_kernel(tc, xt_words, xt_scales, wa_word
         xw = [sb.tile([P, T], U32, name="xw%d" % z, align_bytes=64) for z in range(PASSES)]
         waw = [sb.tile([P, N], U32, name="waw%d" % z, align_bytes=64) for z in range(PASSES)]
         raw = [sb.tile([P, PACK, N], F32, name="raw%d" % z, align_bytes=64) for z in range(PASSES)]
-        bcol = sb.tile([P, HALVES, 8], F32, name="bcol")
+        brow = sb.tile([P, P], F32, name="brow")
         ident = sb.tile([P, P], F32, name="ident")
 
+        nc.gpsimd.memset(brow[:], 0.0)
         nc.gpsimd.memset(xs[:].bitcast(I32), 0)
         nc.vector.memset(was[:].bitcast(I32), 0)
         make_identity(nc, ident[:])
 
         def load_scales(plane, src):
-            for q in range(QUADS):
+            for r in range(4):
                 nc.sync.dma_start(
-                    out=plane[32 * q : 32 * q + 4, :].bitcast(I32).rearrange("r (z c) -> r z c", z=PASSES),
-                    in_=src[:, 4 * q : 4 * q + 4, :].rearrange("z r c -> r z c").bitcast(I32),
+                    out=plane[r:P:32, :].bitcast(I32).rearrange("q (z c) -> q z c", z=PASSES),
+                    in_=src[:, r:16:4, :].rearrange("z q c -> q z c").bitcast(I32),
                 )
 
         def load_words(z):
@@ -61,8 +62,7 @@ def tile_list_rows_onetoken_groupcentred_kernel(tc, xt_words, xt_scales, wa_word
             nc.sync.dma_start(out=raw[z][:], in_=wb[z * 512 : (z + 1) * 512, :].rearrange("(p t) n -> p t n", t=PACK))
 
         nc.sync.dma_start(offsets[:], offs)
-        with nc.allow_non_contiguous_dma(reason="one bias value a partition"):
-            nc.scalar.dma_start(out=bcol[:, :, 0:1], in_=bi.rearrange("o (h p) -> p h o", h=HALVES))
+        nc.scalar.dma_start(out=brow[0:HALVES, :], in_=bi.rearrange("o (h p) -> (o h) p", h=HALVES))
         load_wb(0)
         load_scales(xs, xt_scales)
         load_wb(1)
@@ -71,6 +71,11 @@ def tile_list_rows_onetoken_groupcentred_kernel(tc, xt_words, xt_scales, wa_word
         load_scales(was, wa_scales)
         load_words(1)
         load_wa(1)
+
+        bias_ps = ps.tile([P, N], F32, name="bias_ps", tag="mag1")
+        nc.tensor.transpose(bias_ps[:, 0:P], brow[:], ident[:])
+        bcol = sb.tile([P, HALVES], F32, name="bcol")
+        nc.scalar.copy(bcol[:], bias_ps[:, 0:HALVES])
 
         wbw, wbs, xgs = [], [], []
         for z in range(PASSES):
@@ -96,36 +101,34 @@ def tile_list_rows_onetoken_groupcentred_kernel(tc, xt_words, xt_scales, wa_word
                 jcols = slice(jt * P, (jt + 1) * P)
                 words = sb.tile([P, P], U32, name="xgw%d%d" % (z, jt), align_bytes=64)
                 nc.vector.tensor_copy(words[:], xw[z][:].indirect(offsets[:, jt * 8 : (jt + 1) * 8]))
+                nc.tensor.matmul_mx(
+                    out=acc[jt][:], lhsT=words[:].bitcast(E5M2), lhsT_scale=xgs[z][:, jcols],
+                    rhs=waw[z][:].bitcast(E4M3), rhs_scale=was[:, wcols], start=(z == 0), stop=(z == PASSES - 1),
+                )
                 for h in range(HALVES):
                     cols = slice(h * P, (h + 1) * P)
                     nc.tensor.matmul_mx(
                         out=bT[jt][h][:], lhsT=wbw[z][:, cols].bitcast(E4M3), lhsT_scale=wbs[z][:, cols],
                         rhs=words[:].bitcast(E5M2), rhs_scale=xgs[z][:, jcols], start=(z == 0), stop=(z == PASSES - 1),
                     )
-                nc.tensor.matmul_mx(
-                    out=acc[jt][:], lhsT=words[:].bitcast(E5M2), lhsT_scale=xgs[z][:, jcols],
-                    rhs=waw[z][:].bitcast(E4M3), rhs_scale=was[:, wcols], start=(z == 0), stop=(z == PASSES - 1),
-                )
 
         mag = []
         for jt in range(HALVES):
             turned = ps.tile([P, N], F32, name="mag%d" % jt, tag="mag%d" % jt)
             for h in range(HALVES):
                 m = sb.tile([P, P], F32, name="magT%d%d" % (jt, h))
-                nc.scalar.activation(m[:], bT[jt][h][:], ACT.Abs, bias=bcol[:, h, 0:1])
+                nc.scalar.activation(m[:], bT[jt][h][:], ACT.Abs, bias=bcol[:, h : h + 1])
                 nc.tensor.transpose(turned[:, h * P : (h + 1) * P], m[:], ident[:])
             mag.append(turned)
 
-        sums, centred = [], []
+        centred = []
         for jt in range(HALVES):
-            s = sb.tile([P, G], F32, name="sums%d" % jt)
-            nc.vector.tensor_reduce(s[:], acc[jt][:].rearrange("p (g i) -> p g i", i=GROUP), mybir.AxisListType.X, ALU.add)
-            sums.append(s)
-        for jt in range(HALVES):
+            groups = acc[jt][:].rearrange("p (g i) -> p g i", i=GROUP)
+            sums = sb.tile([P, G], F32, name="sums%d" % jt)
+            nc.vector.tensor_reduce(sums[:], groups, mybir.AxisListType.X, ALU.add)
             c = sb.tile([P, G, GROUP], F32, name="centred%d" % jt)
             nc.vector.scalar_tensor_tensor(
-                c[:], sums[jt][:].unsqueeze(2).to_broadcast([P, G, GROUP]), -1.0 / GROUP,
-                acc[jt][:].rearrange("p (g i) -> p g i", i=GROUP), ALU.mult, ALU.add,
+                c[:], sums[:].unsqueeze(2).to_broadcast([P, G, GROUP]), -1.0 / GROUP, groups, ALU.mult, ALU.add
             )
             centred.append(c)
         for jt in range(HALVES):

from contextlib import ExitStack

import concourse.mybir as mybir
from concourse.masks import make_identity

K, T, J, N, G = 1024, 1024, 256, 256, 32
FLOPS = 2 * 2 * K * J * N

F32 = mybir.dt.float32
BF16 = mybir.dt.bfloat16
I32 = mybir.dt.int32
U32 = mybir.dt.uint32
U16 = mybir.dt.uint16
U8 = mybir.dt.uint8
E4M3 = mybir.dt.float8_e4m3fn_x4
E5M2 = mybir.dt.float8_e5m2_x4
ALU = mybir.AluOpType
ACT = mybir.ActivationFunctionType

P = 128
PACK = 4
PASSES = K // (P * PACK)
HALVES = 2
QUADS = 4
GROUP = N // G


def tile_list_rows_onetoken_groupcentred_kernel(tc, xt_words, xt_scales, wa_words, wa_scales, wb, bi, offs, out):
    nc = tc.nc
    with ExitStack() as ctx:
        sb = ctx.enter_context(tc.tile_pool(name="sb", bufs=1))
        ps = ctx.enter_context(tc.psum_pool(name="ps", bufs=1))

        offsets = sb.tile([P, J // 16], U16, name="offsets")
        xs = sb.tile([P, PASSES * T], U8, name="xs", align_bytes=64)
        was = sb.tile([P, PASSES * N], U8, name="was", align_bytes=64)
        xw = [sb.tile([P, T], U32, name="xw%d" % z, align_bytes=64) for z in range(PASSES)]
        waw = [sb.tile([P, N], U32, name="waw%d" % z, align_bytes=64) for z in range(PASSES)]
        raw = [sb.tile([P, PACK, N], F32, name="raw%d" % z, align_bytes=64) for z in range(PASSES)]
        brow = sb.tile([P, P], F32, name="brow")
        ident = sb.tile([P, P], F32, name="ident")

        nc.gpsimd.memset(brow[:], 0.0)
        nc.gpsimd.memset(xs[:].bitcast(I32), 0)
        nc.vector.memset(was[:].bitcast(I32), 0)
        make_identity(nc, ident[:])

        def load_scales(plane, src):
            for r in range(4):
                nc.sync.dma_start(
                    out=plane[r:P:32, :].bitcast(I32).rearrange("q (z c) -> q z c", z=PASSES),
                    in_=src[:, r:16:4, :].rearrange("z q c -> q z c").bitcast(I32),
                )

        def load_words(z):
            nc.sync.dma_start(out=xw[z][:].bitcast(I32), in_=xt_words[z].rearrange("p c t -> p (c t)").bitcast(I32))

        def load_wa(z):
            nc.sync.dma_start(out=waw[z][:].bitcast(I32), in_=wa_words[z].rearrange("p c t -> p (c t)").bitcast(I32))

        def load_wb(z):
            nc.sync.dma_start(out=raw[z][:], in_=wb[z * 512 : (z + 1) * 512, :].rearrange("(p t) n -> p t n", t=PACK))

        nc.sync.dma_start(offsets[:], offs)
        nc.scalar.dma_start(out=brow[0:HALVES, :], in_=bi.rearrange("o (h p) -> (o h) p", h=HALVES))
        load_wb(0)
        load_scales(xs, xt_scales)
        load_wb(1)
        load_words(0)
        load_wa(0)
        load_scales(was, wa_scales)
        load_words(1)
        load_wa(1)

        bias_ps = ps.tile([P, N], F32, name="bias_ps", tag="mag1")
        nc.tensor.transpose(bias_ps[:, 0:P], brow[:], ident[:])
        bcol = sb.tile([P, HALVES], F32, name="bcol")
        nc.scalar.copy(bcol[:], bias_ps[:, 0:HALVES])

        wbw, wbs, xgs = [], [], []
        for z in range(PASSES):
            plane = sb.tile([P, J], U8, name="xgs%d" % z, align_bytes=64)
            nc.vector.tensor_copy(plane[:], xs[:, z * T : (z + 1) * T].indirect(offsets[:]))
            xgs.append(plane)
        bT = [[ps.tile([P, P], F32, name="bT%d%d" % (jt, h)) for h in range(HALVES)] for jt in range(HALVES)]
        acc = [ps.tile([P, N], F32, name="acc%d" % jt) for jt in range(HALVES)]
        for z in range(PASSES):
            grouped = sb.tile([P, N, PACK], BF16, name="grouped%d" % z, align_bytes=64)
            nc.scalar.activation(
                grouped[:].rearrange("p (c i) t -> p c t i", i=4),
                raw[z][:].rearrange("p t (c i) -> p c t i", i=4),
                ACT.Copy,
            )
            codes = sb.tile([P, N], U32, name="wbw%d" % z, align_bytes=64)
            plane = sb.tile([P, N], U8, name="wbs%d" % z, align_bytes=64)
            nc.vector.quantize_mx(out=codes[:].bitcast(E4M3), scales=plane[:], in_=grouped[:].rearrange("p n t -> p (n t)"))
            wbw.append(codes)
            wbs.append(plane)
            wcols = slice(z * N, (z + 1) * N)
            for jt in range(HALVES):
                jcols = slice(jt * P, (jt + 1) * P)
                words = sb.tile([P, P], U32, name="xgw%d%d" % (z, jt), align_bytes=64)
                nc.vector.tensor_copy(words[:], xw[z][:].indirect(offsets[:, jt * 8 : (jt + 1) * 8]))
                nc.tensor.matmul_mx(
                    out=acc[jt][:], lhsT=words[:].bitcast(E5M2), lhsT_scale=xgs[z][:, jcols],
                    rhs=waw[z][:].bitcast(E4M3), rhs_scale=was[:, wcols], start=(z == 0), stop=(z == PASSES - 1),
                )
                for h in range(HALVES):
                    cols = slice(h * P, (h + 1) * P)
                    nc.tensor.matmul_mx(
                        out=bT[jt][h][:], lhsT=wbw[z][:, cols].bitcast(E4M3), lhsT_scale=wbs[z][:, cols],
                        rhs=words[:].bitcast(E5M2), rhs_scale=xgs[z][:, jcols], start=(z == 0), stop=(z == PASSES - 1),
                    )

        mag = []
        for jt in range(HALVES):
            turned = ps.tile([P, N], F32, name="mag%d" % jt, tag="mag%d" % jt)
            for h in range(HALVES):
                m = sb.tile([P, P], F32, name="magT%d%d" % (jt, h))
                nc.scalar.activation(m[:], bT[jt][h][:], ACT.Abs, bias=bcol[:, h : h + 1])
                nc.tensor.transpose(turned[:, h * P : (h + 1) * P], m[:], ident[:])
            mag.append(turned)

        centred = []
        for jt in range(HALVES):
            groups = acc[jt][:].rearrange("p (g i) -> p g i", i=GROUP)
            sums = sb.tile([P, G], F32, name="sums%d" % jt)
            nc.vector.tensor_reduce(sums[:], groups, mybir.AxisListType.X, ALU.add)
            c = sb.tile([P, G, GROUP], F32, name="centred%d" % jt)
            nc.vector.scalar_tensor_tensor(
                c[:], sums[:].unsqueeze(2).to_broadcast([P, G, GROUP]), -1.0 / GROUP, groups, ALU.mult, ALU.add
            )
            centred.append(c)
        for jt in range(HALVES):
            y = sb.tile([P, N], F32, name="y%d" % jt)
            nc.vector.tensor_tensor(y[:], centred[jt][:].rearrange("p g i -> p (g i)"), mag[jt][:], ALU.mult)
            nc.sync.dma_start(out=out[jt * P : (jt + 1) * P, :], in_=y[:])
